import numpy as np, ml_dtypes
CORES = [1,129,9,137,57,185,105,233,113,241,121,249]
N = 12
import mx_ref
NC, KT, ROOT = 256, 2, 5
BF = ml_dtypes.bfloat16
def setup_inputs(rng):
    def f(*shape):
        return mx_ref.flush((rng.standard_normal(shape, dtype=np.float32) * np.exp2(rng.integers(-2, 3, shape[:-1] + (1,)))).astype(BF))
    return {"w": f(N, 128, KT * 512), "x": f(N, 128, KT * 4 * NC)}
def setup_inputs_blocks(rng):
    d = setup_inputs(rng)
    for k in ("w", "x"): d[k] = mx_ref.spread(d[k], rng, 4)
    return d
def setup_inputs_wide(rng):
    d = setup_inputs(rng)
    for k in ("w", "x"): d[k] = mx_ref.flush((d[k].astype(np.float32) * np.exp2(rng.integers(-8, 9, (N, 1, 1))).astype(np.float32)).astype(BF))
    return d
def setup_inputs_zeros(rng):
    d = setup_inputs(rng); v = d["x"].reshape(N, 128, -1, 4).copy()
    v[np.broadcast_to((rng.random((N, 1, v.shape[2], 1)) < 0.33), v.shape)] = 0
    d["x"] = v.reshape(d["x"].shape)
    return d
def reference(w, x):
    QW = [mx_ref.quantize(w[ROOT][:, 512 * t:512 * t + 512]) for t in range(KT)]
    y = np.zeros((N, 128, NC), np.float32)
    for r in range(N):
        for t in range(KT):
            p = mx_ref.matmul(QW[t], mx_ref.quantize(x[r][:, 4 * NC * t:4 * NC * t + 4 * NC]))
            y[r] = p if t == 0 else y[r] + p
    return {"y": y}

@@ -1,0 +1,140 @@
+from concourse.bass import DstId, RemoteDMATransfer
+from concourse.mybir import dt
+
+SIM_CORES = 256
+KT = 2
+WC = 128
+XC = 256
+
+SCRATCH = {
+    "wb": ("sbuf", [128, KT * 4 * WC], "bfloat16"),
+    "xb": ("sbuf", [128, KT * 4 * XC], "bfloat16"),
+    "wq": ("sbuf", [128, KT * WC], "float8_e4m3fn_x4"),
+    "ws": ("sbuf", [128, KT * WC], "uint8"),
+    "xq": ("sbuf", [128, KT * XC], "float8_e4m3fn_x4"),
+    "xs": ("sbuf", [128, KT * XC], "uint8"),
+    "acc": ("psum", [128, 512], "float32"),
+    "yb": ("sbuf", [128, XC], "float32"),
+}
+SEMAPHORES = ["wl", "wqd", "xl", "xqd", "warr", "sent", "mm", "cp", "st"]
+
+
+def _plan(T, topo):
+    root = T.cores[T.root]
+    dests = [c for c in T.cores if c != root]
+    near = [d for d in dests if topo.may_write(root, d)]
+    far = [d for d in dests if not topo.may_write(root, d)]
+    idle = [c for c in range(SIM_CORES)
+            if c != root and T.rank_of(c) is None
+            and topo.host(c) == topo.host(root) and topo.chip(c) == topo.chip(root)]
+    gate = [c for c in idle if all(topo.may_write(c, d) for d in far)]
+    plain = [c for c in idle if c not in gate]
+    here = topo.die(root)
+    gate_a = [c for c in gate if topo.die(c) == here]
+    gate_b = [c for c in gate if topo.die(c) != here]
+    plain_a = [c for c in plain if topo.die(c) == here]
+    plain_b = [c for c in plain if topo.die(c) != here]
+
+    half = len(far) // 2
+    code_jobs = [(gate_a[0], far[:half]), (gate_b[0], far[half:]),
+                 (plain_a[0], near[0:2]), (plain_b[0], near[2:4])]
+    plane_jobs = [(gate_a[1], far + near[0:1]), (plain_b[1], near[1:])]
+
+    sends = {root: [("s", [h for h, _ in plane_jobs]),
+                    ("c", [h for h, _ in code_jobs]),
+                    ("c", near[4:])]}
+    for h, ds in plane_jobs:
+        sends[h] = [("s", ds)]
+    for h, ds in code_jobs:
+        sends[h] = [("c", ds)]
+    return sends
+
+
+def _mask(topo, core, ds):
+    m = topo.mask(core, ds[0])
+    for d in ds:
+        m &= topo.mask(core, d)
+    return m
+
+
+def _engines(m):
+    return bin(m).count("1")
+
+
+def _issue(g, T, topo, core, jobs):
+    left = 0
+    for kind, ds in jobs:
+        ap = T.wq[:].bitcast(dt.uint8) if kind == "c" else T.ws[:]
+        m = _mask(topo, core, ds)
+        ids = []
+        for d in ds:
+            rid, pid = topo.addr(d, core)
+            ids.append(DstId(rid=rid, pnc=pid))
+        g.remote_dma_fused(
+            [RemoteDMATransfer(dst_ids=ids, dma_engine_mask=m, remote_sem=T.sem.warr,
+                               srcs=[ap], dsts=[ap for _ in ds])],
+            local_sem=T.sem.sent)
+        left += _engines(m)
+    return left
+
+
+def rank_program(g, core, T, topo):
+    sends = _plan(T, topo)
+    rank = T.rank_of(core)
+    root = T.cores[T.root]
+    jobs = sends.get(core, [])
+    if rank is None and not jobs:
+        return
+
+    arrive = 0
+    for s, js in sends.items():
+        for _, ds in js:
+            if core in ds:
+                arrive += _engines(_mask(topo, s, ds))
+
+    if rank is None:
+        g.wait_ge(T.sem.warr, arrive)
+        left = _issue(g, T, topo, core, jobs)
+        g.wait_ge(T.sem.sent, left)
+        return
+
+    left = 0
+    if core == root:
+        g.sync.dma_start(T.wb[:], T.w[:]).then_inc(T.sem.wl, 16)
+    g.sync.dma_start(T.xb[:], T.x[:]).then_inc(T.sem.xl, 16)
+
+    if core == root:
+        g.vector.wait_ge(T.sem.wl, 16)
+        for t in range(KT):
+            g.vector.quantize_mx(T.wq[:, WC * t:WC * (t + 1)], T.ws[:, WC * t:WC * (t + 1)],
+                                 T.wb[:, 4 * WC * t:4 * WC * (t + 1)]).then_inc(T.sem.wqd, 1)
+        g.wait_ge(T.sem.wqd, KT)
+        left = _issue(g, T, topo, core, jobs)
+
+    g.vector.wait_ge(T.sem.xl, 16)
+    for t in range(KT):
+        g.vector.quantize_mx(T.xq[:, XC * t:XC * (t + 1)], T.xs[:, XC * t:XC * (t + 1)],
+                             T.xb[:, 4 * XC * t:4 * XC * (t + 1)]).then_inc(T.sem.xqd, 1)
+
+    g.tensor.wait_ge(T.sem.xqd, KT)
+    if core == root:
+        g.tensor.wait_ge(T.sem.wqd, KT)
+    else:
+        g.tensor.wait_ge(T.sem.warr, arrive)
+    for t in range(KT):
+        mm = g.tensor.matmul_mx(T.acc[:, 0:XC],
+                                T.wq[:, WC * t:WC * (t + 1)], T.ws[:, WC * t:WC * (t + 1)],
+                                T.xq[:, XC * t:XC * (t + 1)], T.xs[:, XC * t:XC * (t + 1)],
+                                t == 0, t == KT - 1)
+    mm.then_inc(T.sem.mm, 1)
+
+    g.vector.wait_ge(T.sem.mm, 1)
+    g.vector.tensor_copy(T.yb[:], T.acc[:, 0:XC]).then_inc(T.sem.cp, 1)
+
+    g.sync.wait_ge(T.sem.cp, 1)
+    if left:
+        g.sync.wait_ge(T.sem.sent, left)
+    g.sync.dma_start(T.y[:], T.yb[:]).then_inc(T.sem.st, 16)
+    g.sync.wait_ge(T.sem.st, 16)
+    if left:
+        g.wait_ge(T.sem.sent, left)

@@ -1,10 +1,12 @@
 from concourse.bass import DstId, RemoteDMATransfer
-from concourse.mybir import dt
+from concourse.mybir import dt, ActivationFunctionType
 
 SIM_CORES = 256
 KT = 2
 WC = 128
 XC = 256
+HC = XC // 2
+BANK = 512
 
 SCRATCH = {
     "wb": ("sbuf", [128, KT * 4 * WC], "bfloat16"),
@@ -13,10 +15,13 @@ SCRATCH = {
     "ws": ("sbuf", [128, KT * WC], "uint8"),
     "xq": ("sbuf", [128, KT * XC], "float8_e4m3fn_x4"),
     "xs": ("sbuf", [128, KT * XC], "uint8"),
-    "acc": ("psum", [128, 512], "float32"),
+    "acc": ("psum", [128, 2 * BANK], "float32"),
     "yb": ("sbuf", [128, XC], "float32"),
 }
-SEMAPHORES = ["wl", "wqd", "xl", "xqd", "warr", "sent", "mm", "cp", "st"]
+SEMAPHORES = ["wl0", "wl1", "wq0", "wq1", "xl", "xqd", "a0", "a1", "aw", "ap", "sent", "mma", "mmb", "cp", "st"]
+
+ARR = {"c0": "a0", "c1": "a1", "cw": "aw", "p": "ap"}
+HOLDS = {"c0": (0,), "c1": (1,), "cw": (0, 1), "p": ()}
 
 
 def _plan(T, topo):
@@ -36,17 +41,16 @@ def _plan(T, topo):
     plain_b = [c for c in plain if topo.die(c) != here]
 
     half = len(far) // 2
-    code_jobs = [(gate_a[0], far[:half]), (gate_b[0], far[half:]),
+    code_jobs = [(gate_b[0], far[half:]), (gate_a[0], far[:half]),
                  (plain_a[0], near[0:2]), (plain_b[0], near[2:4])]
-    plane_jobs = [(gate_a[1], far + near[0:1]), (plain_b[1], near[1:])]
+    plane_jobs = [(gate_b[1], far[3:] + near[0:3]), (plain_b[1], near[3:]), (gate_a[1], far[:3])]
 
-    sends = {root: [("s", [h for h, _ in plane_jobs]),
-                    ("c", [h for h, _ in code_jobs]),
-                    ("c", near[4:])]}
+    coders = [h for h, _ in code_jobs]
+    sends = {root: [("c0", coders), ("p", [h for h, _ in plane_jobs]), ("c1", coders), ("cw", near[4:])]}
     for h, ds in plane_jobs:
-        sends[h] = [("s", ds)]
+        sends[h] = [("p", ds)]
     for h, ds in code_jobs:
-        sends[h] = [("c", ds)]
+        sends[h] = [("c0", ds[:1]), ("cw", ds[1:]), ("c1", ds[:1])]
     return sends
 
 
@@ -61,21 +65,25 @@ def _engines(m):
     return bin(m).count("1")
 
 
-def _issue(g, T, topo, core, jobs):
-    left = 0
-    for kind, ds in jobs:
-        ap = T.wq[:].bitcast(dt.uint8) if kind == "c" else T.ws[:]
-        m = _mask(topo, core, ds)
-        ids = []
-        for d in ds:
-            rid, pid = topo.addr(d, core)
-            ids.append(DstId(rid=rid, pnc=pid))
-        g.remote_dma_fused(
-            [RemoteDMATransfer(dst_ids=ids, dma_engine_mask=m, remote_sem=T.sem.warr,
-                               srcs=[ap], dsts=[ap for _ in ds])],
-            local_sem=T.sem.sent)
-        left += _engines(m)
-    return left
+def _view(T, piece):
+    if piece == "p":
+        return T.ws[:]
+    ts = HOLDS[piece]
+    return T.wq[:, WC * ts[0]:WC * (ts[-1] + 1)].bitcast(dt.uint8)
+
+
+def _send(g, T, topo, core, piece, ds):
+    ap = _view(T, piece)
+    m = _mask(topo, core, ds)
+    ids = []
+    for d in ds:
+        rid, pid = topo.addr(d, core)
+        ids.append(DstId(rid=rid, pnc=pid))
+    g.remote_dma_fused(
+        [RemoteDMATransfer(dst_ids=ids, dma_engine_mask=m, remote_sem=T.sem[ARR[piece]],
+                           srcs=[ap], dsts=[ap for _ in ds])],
+        local_sem=T.sem.sent)
+    return _engines(m)
 
 
 def rank_program(g, core, T, topo):
@@ -86,30 +94,44 @@ def rank_program(g, core, T, topo):
     if rank is None and not jobs:
         return
 
-    arrive = 0
+    arrive = {}
     for s, js in sends.items():
-        for _, ds in js:
+        for piece, ds in js:
             if core in ds:
-                arrive += _engines(_mask(topo, s, ds))
+                arrive[piece] = arrive.get(piece, 0) + _engines(_mask(topo, s, ds))
 
     if rank is None:
-        g.wait_ge(T.sem.warr, arrive)
-        left = _issue(g, T, topo, core, jobs)
+        seen = set()
+        left = 0
+        for piece, ds in jobs:
+            want = [piece] if piece in arrive else ["c%d" % t for t in HOLDS[piece]]
+            for p in want:
+                if p not in seen:
+                    g.wait_ge(T.sem[ARR[p]], arrive[p])
+                    seen.add(p)
+            left += _send(g, T, topo, core, piece, ds)
         g.wait_ge(T.sem.sent, left)
         return
 
     left = 0
     if core == root:
-        g.sync.dma_start(T.wb[:], T.w[:]).then_inc(T.sem.wl, 16)
+        for t in range(KT):
+            g.sync.dma_start(T.wb[:, 4 * WC * t:4 * WC * (t + 1)],
+                             T.w[:, 4 * WC * t:4 * WC * (t + 1)]).then_inc(T.sem["wl%d" % t], 16)
     g.sync.dma_start(T.xb[:], T.x[:]).then_inc(T.sem.xl, 16)
 
     if core == root:
-        g.vector.wait_ge(T.sem.wl, 16)
         for t in range(KT):
+            g.vector.wait_ge(T.sem["wl%d" % t], 16)
             g.vector.quantize_mx(T.wq[:, WC * t:WC * (t + 1)], T.ws[:, WC * t:WC * (t + 1)],
-                                 T.wb[:, 4 * WC * t:4 * WC * (t + 1)]).then_inc(T.sem.wqd, 1)
-        g.wait_ge(T.sem.wqd, KT)
-        left = _issue(g, T, topo, core, jobs)
+                                 T.wb[:, 4 * WC * t:4 * WC * (t + 1)]).then_inc(T.sem["wq%d" % t], 1)
+        packed = 0
+        for piece, ds in jobs:
+            need = KT if piece == "p" else HOLDS[piece][-1] + 1
+            while packed < need:
+                g.wait_ge(T.sem["wq%d" % packed], 1)
+                packed += 1
+            left += _send(g, T, topo, core, piece, ds)
 
     g.vector.wait_ge(T.sem.xl, 16)
     for t in range(KT):
@@ -117,21 +139,31 @@ def rank_program(g, core, T, topo):
                              T.xb[:, 4 * XC * t:4 * XC * (t + 1)]).then_inc(T.sem.xqd, 1)
 
     g.tensor.wait_ge(T.sem.xqd, KT)
-    if core == root:
-        g.tensor.wait_ge(T.sem.wqd, KT)
-    else:
-        g.tensor.wait_ge(T.sem.warr, arrive)
+    if core != root:
+        g.tensor.wait_ge(T.sem.ap, arrive["p"])
     for t in range(KT):
-        mm = g.tensor.matmul_mx(T.acc[:, 0:XC],
-                                T.wq[:, WC * t:WC * (t + 1)], T.ws[:, WC * t:WC * (t + 1)],
-                                T.xq[:, XC * t:XC * (t + 1)], T.xs[:, XC * t:XC * (t + 1)],
-                                t == 0, t == KT - 1)
-    mm.then_inc(T.sem.mm, 1)
+        if core == root:
+            g.tensor.wait_ge(T.sem["wq%d" % t], 1)
+        elif "cw" in arrive:
+            if t == 0:
+                g.tensor.wait_ge(T.sem.aw, arrive["cw"])
+        else:
+            g.tensor.wait_ge(T.sem[ARR["c%d" % t]], arrive["c%d" % t])
+        for h in range(2):
+            lo = XC * t + HC * h
+            mm = g.tensor.matmul_mx(T.acc[:, BANK * h:BANK * h + HC],
+                                    T.wq[:, WC * t:WC * (t + 1)], T.ws[:, WC * t:WC * (t + 1)],
+                                    T.xq[:, lo:lo + HC], T.xs[:, lo:lo + HC],
+                                    t == 0, t == KT - 1)
+            if t == KT - 1:
+                mm.then_inc(T.sem.mma if h == 0 else T.sem.mmb, 1)
 
-    g.vector.wait_ge(T.sem.mm, 1)
-    g.vector.tensor_copy(T.yb[:], T.acc[:, 0:XC]).then_inc(T.sem.cp, 1)
+    g.vector.wait_ge(T.sem.mma, 1)
+    g.vector.tensor_copy(T.yb[:, 0:HC], T.acc[:, 0:HC]).then_inc(T.sem.cp, 1)
+    g.scalar.wait_ge(T.sem.mmb, 1)
+    g.scalar.activation(T.yb[:, HC:XC], T.acc[:, BANK:BANK + HC], ActivationFunctionType.Copy).then_inc(T.sem.cp, 1)
 
-    g.sync.wait_ge(T.sem.cp, 1)
+    g.sync.wait_ge(T.sem.cp, 2)
     if left:
         g.sync.wait_ge(T.sem.sent, left)
     g.sync.dma_start(T.y[:], T.yb[:]).then_inc(T.sem.st, 16)

from concourse.bass import DstId, RemoteDMATransfer
from concourse.mybir import dt, ActivationFunctionType

SIM_CORES = 256
KT = 2
WC = 128
XC = 256
HC = XC // 2
BANK = 512

SCRATCH = {
    "wb": ("sbuf", [128, KT * 4 * WC], "bfloat16"),
    "xb": ("sbuf", [128, KT * 4 * XC], "bfloat16"),
    "wq": ("sbuf", [128, KT * WC], "float8_e4m3fn_x4"),
    "ws": ("sbuf", [128, KT * WC], "uint8"),
    "xq": ("sbuf", [128, KT * XC], "float8_e4m3fn_x4"),
    "xs": ("sbuf", [128, KT * XC], "uint8"),
    "acc": ("psum", [128, 2 * BANK], "float32"),
    "yb": ("sbuf", [128, XC], "float32"),
}
SEMAPHORES = ["wl0", "wl1", "wq0", "wq1", "xl", "xqd", "a0", "a1", "aw", "ap", "sent", "mma", "mmb", "cp", "st"]

ARR = {"c0": "a0", "c1": "a1", "cw": "aw", "p": "ap"}
HOLDS = {"c0": (0,), "c1": (1,), "cw": (0, 1), "p": ()}


def _plan(T, topo):
    root = T.cores[T.root]
    dests = [c for c in T.cores if c != root]
    near = [d for d in dests if topo.may_write(root, d)]
    far = [d for d in dests if not topo.may_write(root, d)]
    idle = [c for c in range(SIM_CORES)
            if c != root and T.rank_of(c) is None
            and topo.host(c) == topo.host(root) and topo.chip(c) == topo.chip(root)]
    gate = [c for c in idle if all(topo.may_write(c, d) for d in far)]
    plain = [c for c in idle if c not in gate]
    here = topo.die(root)
    gate_a = [c for c in gate if topo.die(c) == here]
    gate_b = [c for c in gate if topo.die(c) != here]
    plain_a = [c for c in plain if topo.die(c) == here]
    plain_b = [c for c in plain if topo.die(c) != here]

    half = len(far) // 2
    code_jobs = [(gate_b[0], far[half:]), (gate_a[0], far[:half]),
                 (plain_a[0], near[0:2]), (plain_b[0], near[2:4])]
    plane_jobs = [(gate_b[1], far[3:] + near[0:3]), (plain_b[1], near[3:]), (gate_a[1], far[:3])]

    coders = [h for h, _ in code_jobs]
    sends = {root: [("c0", coders), ("p", [h for h, _ in plane_jobs]), ("c1", coders), ("cw", near[4:])]}
    for h, ds in plane_jobs:
        sends[h] = [("p", ds)]
    for h, ds in code_jobs:
        sends[h] = [("c0", ds[:1]), ("cw", ds[1:]), ("c1", ds[:1])]
    return sends


def _mask(topo, core, ds):
    m = topo.mask(core, ds[0])
    for d in ds:
        m &= topo.mask(core, d)
    return m


def _engines(m):
    return bin(m).count("1")


def _view(T, piece):
    if piece == "p":
        return T.ws[:]
    ts = HOLDS[piece]
    return T.wq[:, WC * ts[0]:WC * (ts[-1] + 1)].bitcast(dt.uint8)


def _send(g, T, topo, core, piece, ds):
    ap = _view(T, piece)
    m = _mask(topo, core, ds)
    ids = []
    for d in ds:
        rid, pid = topo.addr(d, core)
        ids.append(DstId(rid=rid, pnc=pid))
    g.remote_dma_fused(
        [RemoteDMATransfer(dst_ids=ids, dma_engine_mask=m, remote_sem=T.sem[ARR[piece]],
                           srcs=[ap], dsts=[ap for _ in ds])],
        local_sem=T.sem.sent)
    return _engines(m)


def rank_program(g, core, T, topo):
    sends = _plan(T, topo)
    rank = T.rank_of(core)
    root = T.cores[T.root]
    jobs = sends.get(core, [])
    if rank is None and not jobs:
        return

    arrive = {}
    for s, js in sends.items():
        for piece, ds in js:
            if core in ds:
                arrive[piece] = arrive.get(piece, 0) + _engines(_mask(topo, s, ds))

    if rank is None:
        seen = set()
        left = 0
        for piece, ds in jobs:
            want = [piece] if piece in arrive else ["c%d" % t for t in HOLDS[piece]]
            for p in want:
                if p not in seen:
                    g.wait_ge(T.sem[ARR[p]], arrive[p])
                    seen.add(p)
            left += _send(g, T, topo, core, piece, ds)
        g.wait_ge(T.sem.sent, left)
        return

    left = 0
    if core == root:
        for t in range(KT):
            g.sync.dma_start(T.wb[:, 4 * WC * t:4 * WC * (t + 1)],
                             T.w[:, 4 * WC * t:4 * WC * (t + 1)]).then_inc(T.sem["wl%d" % t], 16)
    g.sync.dma_start(T.xb[:], T.x[:]).then_inc(T.sem.xl, 16)

    if core == root:
        for t in range(KT):
            g.vector.wait_ge(T.sem["wl%d" % t], 16)
            g.vector.quantize_mx(T.wq[:, WC * t:WC * (t + 1)], T.ws[:, WC * t:WC * (t + 1)],
                                 T.wb[:, 4 * WC * t:4 * WC * (t + 1)]).then_inc(T.sem["wq%d" % t], 1)
        packed = 0
        for piece, ds in jobs:
            need = KT if piece == "p" else HOLDS[piece][-1] + 1
            while packed < need:
                g.wait_ge(T.sem["wq%d" % packed], 1)
                packed += 1
            left += _send(g, T, topo, core, piece, ds)

    g.vector.wait_ge(T.sem.xl, 16)
    for t in range(KT):
        g.vector.quantize_mx(T.xq[:, XC * t:XC * (t + 1)], T.xs[:, XC * t:XC * (t + 1)],
                             T.xb[:, 4 * XC * t:4 * XC * (t + 1)]).then_inc(T.sem.xqd, 1)

    g.tensor.wait_ge(T.sem.xqd, KT)
    if core != root:
        g.tensor.wait_ge(T.sem.ap, arrive["p"])
    for t in range(KT):
        if core == root:
            g.tensor.wait_ge(T.sem["wq%d" % t], 1)
        elif "cw" in arrive:
            if t == 0:
                g.tensor.wait_ge(T.sem.aw, arrive["cw"])
        else:
            g.tensor.wait_ge(T.sem[ARR["c%d" % t]], arrive["c%d" % t])
        for h in range(2):
            lo = XC * t + HC * h
            mm = g.tensor.matmul_mx(T.acc[:, BANK * h:BANK * h + HC],
                                    T.wq[:, WC * t:WC * (t + 1)], T.ws[:, WC * t:WC * (t + 1)],
                                    T.xq[:, lo:lo + HC], T.xs[:, lo:lo + HC],
                                    t == 0, t == KT - 1)
            if t == KT - 1:
                mm.then_inc(T.sem.mma if h == 0 else T.sem.mmb, 1)

    g.vector.wait_ge(T.sem.mma, 1)
    g.vector.tensor_copy(T.yb[:, 0:HC], T.acc[:, 0:HC]).then_inc(T.sem.cp, 1)
    g.scalar.wait_ge(T.sem.mmb, 1)
    g.scalar.activation(T.yb[:, HC:XC], T.acc[:, BANK:BANK + HC], ActivationFunctionType.Copy).then_inc(T.sem.cp, 1)

    g.sync.wait_ge(T.sem.cp, 2)
    if left:
        g.sync.wait_ge(T.sem.sent, left)
    g.sync.dma_start(T.y[:], T.yb[:]).then_inc(T.sem.st, 16)
    g.sync.wait_ge(T.sem.st, 16)
    if left:
        g.wait_ge(T.sem.sent, left)
